import numpy as np
import ml_dtypes


def mxq(x, axis, fmt="e4m3"):
    dtype, down = {"e4m3": (ml_dtypes.float8_e4m3fn, 7), "e5m2": (ml_dtypes.float8_e5m2, 14)}[fmt]
    v = np.moveaxis(np.asarray(x, np.float32).astype(ml_dtypes.bfloat16).astype(np.float64), axis, -1)
    blocks = v.reshape(v.shape[:-1] + (-1, 32))
    amax = np.abs(blocks).max(-1, keepdims=True)
    byte = np.maximum(np.where(amax > 0, np.frexp(amax)[1] - 1 + 127, 0) - down, 1)
    scale = np.exp2(byte - 127.0)
    codes = (blocks / scale).astype(np.float32).astype(dtype).astype(np.float64)
    return np.moveaxis((codes * scale).reshape(v.shape), -1, axis)


WIDE = False


def mx_kscale(k):
    if not WIDE:
        return np.ones(k)
    levels = np.array([30, -30])
    if k % 512:
        return np.exp2(np.random.permutation(np.resize(levels, k // 32))).repeat(32)
    a = np.empty((k // 512, 16))
    for p in range(k // 512):
        a[p, :8] = np.random.permutation(np.resize(levels, 8))
        for g in range(8):
            far = levels[np.abs(levels - a[p, g]) >= 10]
            a[p, g + 8] = far[np.random.randint(len(far))]
    return np.exp2(a.ravel()).repeat(32)


def f64(x):
    return np.asarray(x).astype(np.float64)


def striped(idx):
    return np.tile(idx.reshape(-1, 16).T, (8, 1)).astype(np.uint16)


def unstriped(offs):
    return offs[:16].T.reshape(-1).astype(np.int64)


E2M1 = np.array([0.0, 0.5, 1.0, 1.5, 2.0, 3.0, 4.0, 6.0, -0.0, -0.5, -1.0, -1.5, -2.0, -3.0, -4.0, -6.0])


def pack_weight(w, fmt):
    k, n = w.shape
    w = f64(np.asarray(w, np.float32).astype(ml_dtypes.bfloat16)).reshape(k // 32, 32, n)
    amax = np.abs(w).max(1)
    if fmt == "e4m3":
        byte = np.frexp(amax)[1] - 1 + 127 - 7
    else:
        mant, ex = np.frexp(amax / 6.0)
        byte = np.where(mant > 0.5, ex, ex - 1) + 127
    byte = np.clip(np.where(amax > 0, byte, 1), 1, 254)
    scaled = (w * np.exp2(127.0 - byte)[:, None, :]).reshape(k, n).astype(np.float32)
    by_word = np.ascontiguousarray(scaled.reshape(k // 512, 128, 4, n).transpose(0, 1, 3, 2))
    if fmt == "e4m3":
        words = by_word.astype(ml_dtypes.float8_e4m3fn).view(np.uint8)
    else:
        c = by_word.astype(ml_dtypes.float4_e2m1fn).view(np.uint8) & 0xF
        words = (c[..., 0::2] | (c[..., 1::2] << 4)).reshape(k // 512, 128, 2 * n)
    return np.ascontiguousarray(words), np.ascontiguousarray(byte.astype(np.uint8).reshape(k // 512, 16, n))


def unpack_weight(words, scales, fmt):
    g, _, n = scales.shape
    words = np.ascontiguousarray(words).reshape(g, 128, n, -1)
    if fmt == "e4m3":
        vals = words.view(ml_dtypes.float8_e4m3fn).astype(np.float64)
    else:
        nib = np.empty((g, 128, n, 4), np.uint8)
        nib[..., 0::2] = words & 0xF
        nib[..., 1::2] = words >> 4
        vals = E2M1[nib]
    vals = vals * np.repeat(np.exp2(scales.astype(np.float64) - 127.0), 8, axis=1)[..., None]
    return vals.transpose(0, 1, 3, 2).reshape(g * 512, n)


def sigmoid(v):
    return 1.0 / (1.0 + np.exp(-np.maximum(v, -700.0)))


def d_sigmoid(v):
    s = 1.0 / (1.0 + np.exp(-np.maximum(v, -700.0)))
    return s * (1.0 - s)


K, T, E, C, H, N = 128, 2048, 8, 512, 512, 512


def by_expert(wq, xq):
    return np.concatenate([wq[e].T @ xq[:, e * C:(e + 1) * C] for e in range(E)], axis=1)


def setup_inputs():
    n = np.random.standard_normal
    s = mx_kscale(N)[:, None]
    u = mx_kscale(H)
    first = np.random.permutation(np.repeat(np.arange(E), T // E))
    second = (first + 1 + np.random.permutation(np.repeat(np.arange(E - 1), -(-T // (E - 1)))[:T])) % E
    while np.bincount(second, minlength=E).max() != T // E:
        load = np.bincount(second, minlength=E); hi, lo = int(load.argmax()), int(load.argmin())
        t = np.flatnonzero((second == hi) & (first != lo))[0]; second[t] = lo
    slot_token = np.empty(E * C, np.int64); pos = np.empty((2, T), np.int64); fill = np.zeros(E, np.int64)
    place = np.stack([np.random.permutation(C) for _ in range(E)])
    for r, deal in enumerate((first, second)):
        for t in np.random.permutation(T):
            e = deal[t]; j = e * C + place[e, fill[e]]; fill[e] += 1; slot_token[j] = t; pos[r, t] = j
    g = np.random.uniform(0.2, 0.8, T)
    w_slot = np.empty(E * C); w_slot[pos[0]] = g; w_slot[pos[1]] = 1.0 - g
    w2 = [pack_weight(m, "e2m1") for m in n((E, N, H)) / np.sqrt(N) / s[None] * u[None, None, :]]
    w1 = [pack_weight(m, "e2m1") for m in n((E, H, K)) / np.sqrt(H) / u[None, :, None]]
    w3 = [pack_weight(m, "e2m1") for m in n((E, H, K)) / np.sqrt(H) / u[None, :, None]]
    return {
        "dyT": (n((N, T)) * s).astype(np.float32),
        "a1": n((H, E * C)).astype(np.float32),
        "a3": n((H, E * C)).astype(np.float32),
        "w2_words": np.stack([m[0] for m in w2]),
        "w2_scales": np.stack([m[1] for m in w2]),
        "w1_words": np.stack([m[0] for m in w1]),
        "w1_scales": np.stack([m[1] for m in w1]),
        "w3_words": np.stack([m[0] for m in w3]),
        "w3_scales": np.stack([m[1] for m in w3]),
        "gate": np.tile(w_slot, (N, 1)).astype(np.float32),
        "offs": striped(slot_token),
        "pos1": striped(pos[0]),
        "pos2": striped(pos[1]),
    }


def reference(dyT, a1, a3, w2_words, w2_scales, w1_words, w1_scales, w3_words, w3_scales, gate, offs, pos1, pos2):
    idx = unstriped(offs)
    w2 = np.stack([unpack_weight(w2_words[e], w2_scales[e], "e2m1") for e in range(E)])
    w1 = np.stack([unpack_weight(w1_words[e], w1_scales[e], "e2m1") for e in range(E)])
    w3 = np.stack([unpack_weight(w3_words[e], w3_scales[e], "e2m1") for e in range(E)])
    gq = mxq(f64(gate) * f64(dyT)[:, idx], 0, "e5m2")
    dh = by_expert(w2, gq)
    da1 = dh * f64(a3) * d_sigmoid(f64(a1))
    da3 = dh * sigmoid(f64(a1))
    dx = by_expert(w1, mxq(da1, 0, "e5m2")) + by_expert(w3, mxq(da3, 0, "e5m2"))
    return dx[:, unstriped(pos1)] + dx[:, unstriped(pos2)]

@@ -1,0 +1,267 @@
+from contextlib import ExitStack
+
+import concourse.mybir as mybir
+
+F32 = mybir.dt.float32
+BF16 = mybir.dt.bfloat16
+I32 = mybir.dt.int32
+U32 = mybir.dt.uint32
+U16 = mybir.dt.uint16
+U8 = mybir.dt.uint8
+E5M2X4 = mybir.dt.float8_e5m2_x4
+E2M1X4 = mybir.dt.float4_e2m1fn_x4
+
+MULT = mybir.AluOpType.mult
+ADD = mybir.AluOpType.add
+SUB = mybir.AluOpType.subtract
+SIGMOID = mybir.ActivationFunctionType.Sigmoid
+
+P = 128
+K, T, E, C, H, N = 128, 2048, 8, 512, 512, 512
+S = E * C
+PACK = 4
+
+FLOPS = 2 * S * (N * H + 2 * H * K)
+BYTES = 4 * (N * T + 2 * H * S + S + K * T) + E * (N * H + 2 * H * K) * 17 // 32 + 2 * P * (S + 2 * T) // 16
+
+
+def planes(ap):
+    return ap.rearrange("p t (c i) -> p c t i", i=4)
+
+
+def woven(ap):
+    return ap.rearrange("p (c i) t -> p c t i", i=4)
+
+
+def tile_moe_bdx_glu_sigmoid_kernel(
+    tc, dyT, a1, a3, w2_words, w2_scales, w1_words, w1_scales, w3_words, w3_scales, gate, offs, pos1, pos2, out
+):
+    nc = tc.nc
+    with ExitStack() as ctx:
+        lists = ctx.enter_context(tc.tile_pool(name="lists", bufs=1))
+        held = ctx.enter_context(tc.tile_pool(name="held", bufs=1))
+        acts = ctx.enter_context(tc.tile_pool(name="acts", bufs=3))
+        ring = ctx.enter_context(tc.tile_pool(name="ring", bufs=2))
+        psum_h = ctx.enter_context(tc.psum_pool(name="psum_h", bufs=6))
+        psum_x = ctx.enter_context(tc.psum_pool(name="psum_x", bufs=2))
+
+        l_offs = lists.tile([P, S // 16], U16, name="l_offs")
+        l_pos1 = lists.tile([P, T // 16], U16, name="l_pos1")
+        l_pos2 = lists.tile([P, T // 16], U16, name="l_pos2")
+
+        dy = [held.tile([P, T], F32, name=f"dy{t}") for t in range(PACK)]
+        gates = held.tile([P, S], F32, name="gates")
+        dx = held.tile([P, S], F32, name="dx")
+        w2_sraw = held.tile([P, E * H], U8, align_bytes=64, name="w2_sraw")
+        w2_w = held.tile([P, E * 2 * H], U8, align_bytes=64, name="w2_w")
+        w2_s = held.tile([P, E * H], U8, align_bytes=64, name="w2_s")
+        w13_w = held.tile([P, 2 * E * 2 * K], U8, align_bytes=64, name="w13_w")
+        w13_s = held.tile([P, 2 * E * K], U8, align_bytes=64, name="w13_s")
+
+        nc.gpsimd.memset(w2_sraw[:].bitcast(I32), 0)
+        nc.gpsimd.memset(w13_s[:].bitcast(I32), 0)
+
+        nc.sync.dma_start(l_offs[:], offs)
+        dy_rows = dyT.rearrange("(p t) c -> p t c", t=PACK)
+
+        def load_gate(q):
+            cols = slice(q * 1024, (q + 1) * 1024)
+            nc.sync.dma_start(gates[:, cols], gate[0:P, cols])
+
+        nc.sync.dma_start(dy[0][:], dy_rows[:, 0, :])
+        load_gate(0)
+
+        w2s_view = w2_sraw[:].bitcast(I32).rearrange("p (e i) -> p e i", e=E)
+        w2s_dram = w2_scales.bitcast(I32)
+        for q in range(4):
+            nc.scalar.dma_start(
+                w2s_view[32 * q : 32 * q + 4], w2s_dram[:, 0, 4 * q : 4 * q + 4, :].rearrange("e f i -> f e i")
+            )
+        w2_raws = {}
+
+        def load_w2(pair, queue):
+            raw = ring.tile([P, 2 * 2 * H], U8, align_bytes=64, name="w2_raw")
+            queue.dma_start(
+                raw[:].bitcast(I32).rearrange("p (e i) -> p e i", e=2),
+                w2_words.bitcast(I32)[2 * pair : 2 * pair + 2, 0].rearrange("e p i -> p e i"),
+            )
+            w2_raws[pair] = raw
+
+        load_w2(0, nc.scalar)
+        for t in range(1, PACK):
+            nc.sync.dma_start(dy[t][:], dy_rows[:, t, :])
+
+        a1_rows = a1.rearrange("(p t) c -> p t c", t=PACK)
+        a3_rows = a3.rearrange("(p t) c -> p t c", t=PACK)
+        s_tiles = {}
+        y_tiles = {}
+
+        def load_acts(e):
+            cols = slice(e * C, (e + 1) * C)
+            s_t = acts.tile([P, PACK, C], F32, name="s_t")
+            nc.sync.dma_start(s_t[:], a1_rows[:, :, cols])
+            y_t = acts.tile([P, PACK, C], F32, name="y_t")
+            nc.sync.dma_start(y_t[:], a3_rows[:, :, cols])
+            s_tiles[e] = s_t
+            y_tiles[e] = y_t
+
+        load_acts(0)
+        w13w_view = w13_w[:].bitcast(I32).rearrange("p (w e i) -> p w e i", w=2, e=E)
+        w13s_view = w13_s[:].bitcast(I32).rearrange("p (w e i) -> p w e i", w=2, e=E)
+        for w, (words, scales) in enumerate(((w1_words, w1_scales), (w3_words, w3_scales))):
+            nc.sync.dma_start(w13w_view[:, w], words.bitcast(I32)[:, 0].rearrange("e p i -> p e i"))
+            s_dram = scales.bitcast(I32)
+            for q in range(4):
+                nc.sync.dma_start(
+                    w13s_view[32 * q : 32 * q + 4, w], s_dram[:, 0, 4 * q : 4 * q + 4, :].rearrange("e f i -> f e i")
+                )
+        load_gate(1)
+        load_w2(1, nc.sync)
+        load_acts(1)
+        nc.sync.dma_start(l_pos1[:], pos1)
+        nc.sync.dma_start(l_pos2[:], pos2)
+
+        for e0 in range(0, E, 2):
+            cs = slice(e0 * H, (e0 + 2) * H)
+            nc.gpsimd.tensor_copy(
+                w2_s[:, cs].rearrange("p (e t m) -> p e t m", e=2, t=PACK),
+                w2_sraw[:, cs].rearrange("p (e m t) -> p e t m", e=2, t=PACK),
+            )
+        def permute_words(pair):
+            cs = slice(pair * 4 * H, (pair + 1) * 4 * H)
+            nc.vector.tensor_copy(
+                w2_w[:, cs].bitcast(U16).rearrange("p (e t m) -> p e t m", e=2, t=PACK),
+                w2_raws[pair][:].bitcast(U16).rearrange("p (e m t) -> p e t m", e=2, t=PACK),
+            )
+
+        g32s = {}
+        codes = {}
+        banks = {}
+        da3s = {}
+        packed = {}
+
+        def new_g32(e):
+            g32 = ring.tile([P, PACK, C], F32, bufs=3, name="g32")
+            g32s[e] = g32
+
+        def gather(e, t):
+            nc.vector.tensor_tensor(
+                g32s[e][:, t, :],
+                dy[t][:].indirect(l_offs[:, e * C // 16 : (e + 1) * C // 16]),
+                gates[:, e * C : (e + 1) * C],
+                MULT,
+            )
+
+        def weave_g(e):
+            gb = ring.tile([P, C, PACK], BF16, align_bytes=64, name="gb")
+            nc.scalar.copy(woven(gb[:]), planes(g32s[e][:]))
+            packed[e] = gb
+
+        def quantize(src, name):
+            cd = ring.tile([P, C], U32, align_bytes=64, name=f"c_{name}")
+            sc = ring.tile([P, C], U8, align_bytes=64, name=f"s_{name}")
+            nc.vector.quantize_mx(
+                out=cd[:].bitcast(E5M2X4), scales=sc[:], in_=src[:].rearrange("p c t -> p (c t)")
+            )
+            return cd, sc
+
+        def first_product(e):
+            cd, sc = quantize(packed[e], "g")
+            out_banks = []
+            for t in range(PACK):
+                bank = psum_h.tile([P, C], F32, name="bank")
+                w0 = e * 2 * H + t * 2 * P
+                s0 = e * H + t * P
+                nc.tensor.matmul_mx(
+                    out=bank[:],
+                    lhsT=w2_w[:, w0 : w0 + 2 * P].bitcast(E2M1X4),
+                    lhsT_scale=w2_s[:, s0 : s0 + P],
+                    rhs=cd[:].bitcast(E5M2X4),
+                    rhs_scale=sc[:],
+                    start=True,
+                    stop=True,
+                )
+                out_banks.append(bank)
+            banks[e] = out_banks
+
+        def sig(e):
+            nc.scalar.activation(s_tiles[e][:], s_tiles[e][:], SIGMOID, scale=-1.0)
+
+        def make_y(e):
+            nc.vector.tensor_tensor(y_tiles[e][:], s_tiles[e][:], y_tiles[e][:], MULT)
+
+        def make_da3(e):
+            d3 = ring.tile([P, PACK, C], F32, name="d3")
+            for t in range(PACK):
+                nc.vector.scalar_tensor_tensor(d3[:, t, :], s_tiles[e][:, t, :], 1.0, banks[e][t][:], SUB, MULT)
+            d3b = ring.tile([P, C, PACK], BF16, align_bytes=64, name="d3b")
+            nc.scalar.copy(woven(d3b[:]), planes(d3[:]))
+            da3s[e] = (d3, d3b)
+
+        def make_da1(e):
+            d1b = ring.tile([P, C, PACK], BF16, align_bytes=64, name="d1b")
+            nc.vector.tensor_tensor(woven(d1b[:]), planes(y_tiles[e][:]), planes(da3s[e][0][:]), MULT)
+            packed[e] = d1b
+
+        def second_product(e):
+            acc = psum_x.tile([P, C], F32, name="acc")
+            for w, (src, name) in enumerate(((packed[e], "d1"), (da3s[e][1], "d3"))):
+                cd, sc = quantize(src, name)
+                w0 = (w * E + e) * 2 * K
+                s0 = (w * E + e) * K
+                nc.tensor.matmul_mx(
+                    out=acc[:],
+                    lhsT=w13_w[:, w0 : w0 + 2 * K].bitcast(E2M1X4),
+                    lhsT_scale=w13_s[:, s0 : s0 + K],
+                    rhs=cd[:].bitcast(E5M2X4),
+                    rhs_scale=sc[:],
+                    start=(w == 0),
+                    stop=(w == 1),
+                )
+            nc.scalar.activation(dx[:, e * C : (e + 1) * C], acc[:], mybir.ActivationFunctionType.Copy, scale=-1.0)
+
+        new_g32(0)
+        new_g32(1)
+        for t in range(PACK):
+            gather(0, t)
+            gather(1, t)
+        permute_words(0)
+        weave_g(0)
+        sig(0)
+        first_product(0)
+        weave_g(1)
+        make_y(0)
+
+        for e in range(E):
+            if e + 2 < E:
+                load_acts(e + 2)
+                if e in (0, 2):
+                    load_gate(e // 2 + 2)
+                    load_w2(e // 2 + 2, nc.sync)
+            if e % 2 == 1 and e + 1 < E:
+                permute_words((e + 1) // 2)
+            make_da3(e)
+            if e + 2 < E:
+                new_g32(e + 2)
+                gather(e + 2, 0)
+                gather(e + 2, 1)
+            make_da1(e)
+            if e + 1 < E:
+                sig(e + 1)
+                first_product(e + 1)
+            if e + 2 < E:
+                gather(e + 2, 2)
+                gather(e + 2, 3)
+                weave_g(e + 2)
+            second_product(e)
+            if e + 1 < E:
+                make_y(e + 1)
+
+        for c in range(T // C):
+            ls = slice(c * C // 16, (c + 1) * C // 16)
+            r = ring.tile([P, PACK, C], F32, bufs=3, name="g32")
+            nc.vector.tensor_copy(r[:, 0, :], dx[:].indirect(l_pos1[:, ls]))
+            nc.vector.tensor_copy(r[:, 1, :], dx[:].indirect(l_pos2[:, ls]))
+            eng = nc.vector if c == T // C - 1 else nc.gpsimd
+            eng.tensor_tensor(r[:, 2, :], r[:, 0, :], r[:, 1, :], ADD)
+            nc.sync.dma_start(out[:, c * C : (c + 1) * C], r[:, 2, :])

@@ -20,6 +20,7 @@ P = 128
 K, T, E, C, H, N = 128, 2048, 8, 512, 512, 512
 S = E * C
 PACK = 4
+Y_SPLIT = 2
 
 FLOPS = 2 * S * (N * H + 2 * H * K)
 BYTES = 4 * (N * T + 2 * H * S + S + K * T) + E * (N * H + 2 * H * K) * 17 // 32 + 2 * P * (S + 2 * T) // 16
@@ -64,12 +65,14 @@ def tile_moe_bdx_glu_sigmoid_kernel(
         nc.sync.dma_start(l_offs[:], offs)
         dy_rows = dyT.rearrange("(p t) c -> p t c", t=PACK)
 
-        def load_gate(q):
-            cols = slice(q * 1024, (q + 1) * 1024)
+        def load_gate(e, count):
+            cols = slice(e * C, (e + count) * C)
             nc.sync.dma_start(gates[:, cols], gate[0:P, cols])
 
+        load_gate(0, 1)
         nc.sync.dma_start(dy[0][:], dy_rows[:, 0, :])
-        load_gate(0)
+        load_gate(1, 1)
+        load_gate(2, 1)
 
         w2s_view = w2_sraw[:].bitcast(I32).rearrange("p (e i) -> p e i", e=E)
         w2s_dram = w2_scales.bitcast(I32)
@@ -88,22 +91,25 @@ def tile_moe_bdx_glu_sigmoid_kernel(
             w2_raws[pair] = raw
 
         load_w2(0, nc.scalar)
-        for t in range(1, PACK):
+        for t in range(1, PACK - 1):
             nc.sync.dma_start(dy[t][:], dy_rows[:, t, :])
 
         a1_rows = a1.rearrange("(p t) c -> p t c", t=PACK)
         a3_rows = a3.rearrange("(p t) c -> p t c", t=PACK)
         s_tiles = {}
+        a3_tiles = {}
         y_tiles = {}
 
         def load_acts(e):
             cols = slice(e * C, (e + 1) * C)
             s_t = acts.tile([P, PACK, C], F32, name="s_t")
             nc.sync.dma_start(s_t[:], a1_rows[:, :, cols])
-            y_t = acts.tile([P, PACK, C], F32, name="y_t")
-            nc.sync.dma_start(y_t[:], a3_rows[:, :, cols])
+            if e == 0:
+                nc.sync.dma_start(dy[PACK - 1][:], dy_rows[:, PACK - 1, :])
+            a3_t = acts.tile([P, PACK, C], F32, bufs=2, name="a3_t")
+            nc.sync.dma_start(a3_t[:], a3_rows[:, :, cols])
             s_tiles[e] = s_t
-            y_tiles[e] = y_t
+            a3_tiles[e] = a3_t
 
         load_acts(0)
         w13w_view = w13_w[:].bitcast(I32).rearrange("p (w e i) -> p w e i", w=2, e=E)
@@ -115,18 +121,17 @@ def tile_moe_bdx_glu_sigmoid_kernel(
                 nc.sync.dma_start(
                     w13s_view[32 * q : 32 * q + 4, w], s_dram[:, 0, 4 * q : 4 * q + 4, :].rearrange("e f i -> f e i")
                 )
-        load_gate(1)
         load_w2(1, nc.sync)
+        load_gate(3, 1)
         load_acts(1)
         nc.sync.dma_start(l_pos1[:], pos1)
         nc.sync.dma_start(l_pos2[:], pos2)
 
-        for e0 in range(0, E, 2):
-            cs = slice(e0 * H, (e0 + 2) * H)
-            nc.gpsimd.tensor_copy(
-                w2_s[:, cs].rearrange("p (e t m) -> p e t m", e=2, t=PACK),
-                w2_sraw[:, cs].rearrange("p (e m t) -> p e t m", e=2, t=PACK),
-            )
+        nc.vector.tensor_copy(
+            w2_s[:].rearrange("p (e t m) -> p e t m", e=E, t=PACK),
+            w2_sraw[:].rearrange("p (e m t) -> p e t m", e=E, t=PACK),
+        )
+
         def permute_words(pair):
             cs = slice(pair * 4 * H, (pair + 1) * 4 * H)
             nc.vector.tensor_copy(
@@ -157,16 +162,14 @@ def tile_moe_bdx_glu_sigmoid_kernel(
             nc.scalar.copy(woven(gb[:]), planes(g32s[e][:]))
             packed[e] = gb
 
-        def quantize(src, name):
-            cd = ring.tile([P, C], U32, align_bytes=64, name=f"c_{name}")
-            sc = ring.tile([P, C], U8, align_bytes=64, name=f"s_{name}")
-            nc.vector.quantize_mx(
-                out=cd[:].bitcast(E5M2X4), scales=sc[:], in_=src[:].rearrange("p c t -> p (c t)")
-            )
+        def quantize(values, name):
+            cd = ring.tile([P, values.shape[1] // PACK], U32, align_bytes=64, name=f"c_{name}")
+            sc = ring.tile([P, values.shape[1] // PACK], U8, align_bytes=64, name=f"s_{name}")
+            nc.vector.quantize_mx(out=cd[:].bitcast(E5M2X4), scales=sc[:], in_=values)
             return cd, sc
 
         def first_product(e):
-            cd, sc = quantize(packed[e], "g")
+            cd, sc = quantize(packed[e][:].rearrange("p c t -> p (c t)"), "g")
             out_banks = []
             for t in range(PACK):
                 bank = psum_h.tile([P, C], F32, name="bank")
@@ -188,33 +191,38 @@ def tile_moe_bdx_glu_sigmoid_kernel(
             nc.scalar.activation(s_tiles[e][:], s_tiles[e][:], SIGMOID, scale=-1.0)
 
         def make_y(e):
-            nc.vector.tensor_tensor(y_tiles[e][:], s_tiles[e][:], y_tiles[e][:], MULT)
+            y_t = acts.tile([P, PACK, C], F32, bufs=2, name="y_t")
+            y_tiles[e] = y_t
+            split = 0 if e == 0 else Y_SPLIT
+            if split:
+                nc.gpsimd.tensor_tensor(y_t[:, :split, :], s_tiles[e][:, :split, :], a3_tiles[e][:, :split, :], MULT)
+            nc.vector.tensor_tensor(y_t[:, split:, :], s_tiles[e][:, split:, :], a3_tiles[e][:, split:, :], MULT)
 
         def make_da3(e):
             d3 = ring.tile([P, PACK, C], F32, name="d3")
             for t in range(PACK):
                 nc.vector.scalar_tensor_tensor(d3[:, t, :], s_tiles[e][:, t, :], 1.0, banks[e][t][:], SUB, MULT)
-            d3b = ring.tile([P, C, PACK], BF16, align_bytes=64, name="d3b")
-            nc.scalar.copy(woven(d3b[:]), planes(d3[:]))
-            da3s[e] = (d3, d3b)
+            db = ring.tile([P, 2, C, PACK], BF16, align_bytes=64, name="db")
+            nc.scalar.copy(woven(db[:, 1]), planes(d3[:]))
+            da3s[e] = (d3, db)
 
         def make_da1(e):
-            d1b = ring.tile([P, C, PACK], BF16, align_bytes=64, name="d1b")
-            nc.vector.tensor_tensor(woven(d1b[:]), planes(y_tiles[e][:]), planes(da3s[e][0][:]), MULT)
-            packed[e] = d1b
+            d3, db = da3s[e]
+            nc.vector.tensor_tensor(woven(db[:, 0]), planes(y_tiles[e][:]), planes(d3[:]), MULT)
 
         def second_product(e):
             acc = psum_x.tile([P, C], F32, name="acc")
-            for w, (src, name) in enumerate(((packed[e], "d1"), (da3s[e][1], "d3"))):
-                cd, sc = quantize(src, name)
+            cd, sc = quantize(da3s[e][1][:].rearrange("p w c t -> p (w c t)"), "d")
+            for w in range(2):
+                cs = slice(w * C, (w + 1) * C)
                 w0 = (w * E + e) * 2 * K
                 s0 = (w * E + e) * K
                 nc.tensor.matmul_mx(
                     out=acc[:],
                     lhsT=w13_w[:, w0 : w0 + 2 * K].bitcast(E2M1X4),
                     lhsT_scale=w13_s[:, s0 : s0 + K],
-                    rhs=cd[:].bitcast(E5M2X4),
-                    rhs_scale=sc[:],
+                    rhs=cd[:, cs].bitcast(E5M2X4),
+                    rhs_scale=sc[:, cs],
                     start=(w == 0),
                     stop=(w == 1),
                 )
@@ -222,9 +230,10 @@ def tile_moe_bdx_glu_sigmoid_kernel(
 
         new_g32(0)
         new_g32(1)
+        new_g32(2)
         for t in range(PACK):
-            gather(0, t)
-            gather(1, t)
+            for e in range(3):
+                gather(e, t)
         permute_words(0)
         weave_g(0)
         sig(0)
@@ -232,30 +241,31 @@ def tile_moe_bdx_glu_sigmoid_kernel(
         weave_g(1)
         make_y(0)
 
-        for e in range(E):
+        for e in range(E + 1):
+            if e >= 1:
+                make_da1(e - 1)
             if e + 2 < E:
                 load_acts(e + 2)
                 if e in (0, 2):
-                    load_gate(e // 2 + 2)
+                    load_gate(e + 4, 2)
                     load_w2(e // 2 + 2, nc.sync)
-            if e % 2 == 1 and e + 1 < E:
-                permute_words((e + 1) // 2)
-            make_da3(e)
-            if e + 2 < E:
-                new_g32(e + 2)
-                gather(e + 2, 0)
-                gather(e + 2, 1)
-            make_da1(e)
+            if e < E:
+                make_da3(e)
             if e + 1 < E:
                 sig(e + 1)
-                first_product(e + 1)
-            if e + 2 < E:
-                gather(e + 2, 2)
-                gather(e + 2, 3)
-                weave_g(e + 2)
-            second_product(e)
-            if e + 1 < E:
                 make_y(e + 1)
+            if e >= 1:
+                second_product(e - 1)
+            if e + 3 < E:
+                new_g32(e + 3)
+                for t in range(PACK):
+                    gather(e + 3, t)
+            if e + 2 < E:
+                weave_g(e + 2)
+            if e % 2 == 1 and e + 1 < E:
+                permute_words((e + 1) // 2)
+            if e + 1 < E:
+                first_product(e + 1)
 
         for c in range(T // C):
             ls = slice(c * C // 16, (c + 1) * C // 16)

@@ -14,13 +14,14 @@ E2M1X4 = mybir.dt.float4_e2m1fn_x4
 MULT = mybir.AluOpType.mult
 ADD = mybir.AluOpType.add
 SUB = mybir.AluOpType.subtract
+COPY = mybir.ActivationFunctionType.Copy
 SIGMOID = mybir.ActivationFunctionType.Sigmoid
 
 P = 128
 K, T, E, C, H, N = 128, 2048, 8, 512, 512, 512
 S = E * C
 PACK = 4
-Y_SPLIT = 2
+Y_GPSIMD = 4
 
 FLOPS = 2 * S * (N * H + 2 * H * K)
 BYTES = 4 * (N * T + 2 * H * S + S + K * T) + E * (N * H + 2 * H * K) * 17 // 32 + 2 * P * (S + 2 * T) // 16
@@ -65,14 +66,14 @@ def tile_moe_bdx_glu_sigmoid_kernel(
         nc.sync.dma_start(l_offs[:], offs)
         dy_rows = dyT.rearrange("(p t) c -> p t c", t=PACK)
 
-        def load_gate(e, count):
-            cols = slice(e * C, (e + count) * C)
+        def load_gate(e):
+            cols = slice(e * C, (e + 1) * C)
             nc.sync.dma_start(gates[:, cols], gate[0:P, cols])
 
-        load_gate(0, 1)
+        load_gate(0)
         nc.sync.dma_start(dy[0][:], dy_rows[:, 0, :])
-        load_gate(1, 1)
-        load_gate(2, 1)
+        load_gate(1)
+        load_gate(2)
 
         w2s_view = w2_sraw[:].bitcast(I32).rearrange("p (e i) -> p e i", e=E)
         w2s_dram = w2_scales.bitcast(I32)
@@ -122,15 +123,17 @@ def tile_moe_bdx_glu_sigmoid_kernel(
                     w13s_view[32 * q : 32 * q + 4, w], s_dram[:, 0, 4 * q : 4 * q + 4, :].rearrange("e f i -> f e i")
                 )
         load_w2(1, nc.sync)
-        load_gate(3, 1)
+        load_gate(3)
         load_acts(1)
         nc.sync.dma_start(l_pos1[:], pos1)
         nc.sync.dma_start(l_pos2[:], pos2)
 
-        nc.vector.tensor_copy(
-            w2_s[:].rearrange("p (e t m) -> p e t m", e=E, t=PACK),
-            w2_sraw[:].rearrange("p (e m t) -> p e t m", e=E, t=PACK),
-        )
+        def permute_scales(e0, e1):
+            cs = slice(e0 * H, e1 * H)
+            nc.vector.tensor_copy(
+                w2_s[:, cs].rearrange("p (e t m) -> p e t m", e=e1 - e0, t=PACK),
+                w2_sraw[:, cs].rearrange("p (e m t) -> p e t m", e=e1 - e0, t=PACK),
+            )
 
         def permute_words(pair):
             cs = slice(pair * 4 * H, (pair + 1) * 4 * H)
@@ -144,6 +147,7 @@ def tile_moe_bdx_glu_sigmoid_kernel(
         banks = {}
         da3s = {}
         packed = {}
+        accs = {}
 
         def new_g32(e):
             g32 = ring.tile([P, PACK, C], F32, bufs=3, name="g32")
@@ -159,8 +163,8 @@ def tile_moe_bdx_glu_sigmoid_kernel(
 
         def weave_g(e):
             gb = ring.tile([P, C, PACK], BF16, align_bytes=64, name="gb")
-            nc.scalar.copy(woven(gb[:]), planes(g32s[e][:]))
             packed[e] = gb
+            nc.scalar.copy(woven(gb[:]), planes(g32s[e][:]))
 
         def quantize(values, name):
             cd = ring.tile([P, values.shape[1] // PACK], U32, align_bytes=64, name=f"c_{name}")
@@ -193,10 +197,10 @@ def tile_moe_bdx_glu_sigmoid_kernel(
         def make_y(e):
             y_t = acts.tile([P, PACK, C], F32, bufs=2, name="y_t")
             y_tiles[e] = y_t
-            split = 0 if e == 0 else Y_SPLIT
-            if split:
-                nc.gpsimd.tensor_tensor(y_t[:, :split, :], s_tiles[e][:, :split, :], a3_tiles[e][:, :split, :], MULT)
-            nc.vector.tensor_tensor(y_t[:, split:, :], s_tiles[e][:, split:, :], a3_tiles[e][:, split:, :], MULT)
+            for t in range(0, PACK, 2):
+                ts = slice(t, t + 2)
+                eng = nc.gpsimd if t < Y_GPSIMD else nc.vector
+                eng.tensor_tensor(y_t[:, ts, :], s_tiles[e][:, ts, :], a3_tiles[e][:, ts, :], MULT)
 
         def make_da3(e):
             d3 = ring.tile([P, PACK, C], F32, name="d3")
@@ -226,52 +230,76 @@ def tile_moe_bdx_glu_sigmoid_kernel(
                     start=(w == 0),
                     stop=(w == 1),
                 )
-            nc.scalar.activation(dx[:, e * C : (e + 1) * C], acc[:], mybir.ActivationFunctionType.Copy, scale=-1.0)
+            accs[e] = acc
 
-        new_g32(0)
-        new_g32(1)
-        new_g32(2)
+        def store_dx(e):
+            nc.scalar.activation(dx[:, e * C : (e + 1) * C], accs[e][:], COPY, scale=-1.0)
+
+        permute_scales(0, E)
+        for e in range(3):
+            new_g32(e)
         for t in range(PACK):
             for e in range(3):
                 gather(e, t)
+        sig(0)
         permute_words(0)
         weave_g(0)
-        sig(0)
+        make_y(0)
         first_product(0)
         weave_g(1)
-        make_y(0)
+        sig(1)
 
+        todo = [(e, t) for e in range(3, E) for t in range(PACK)]
+
+        def gather_some(count):
+            for e, t in todo[:count]:
+                if t == 0:
+                    new_g32(e)
+                gather(e, t)
+            del_count = min(count, len(todo))
+            for i in range(del_count):
+                todo.remove(todo[0])
+
+        quota = (4, 3, 3, 3, 3, 4, 0, 0, 0)
         for e in range(E + 1):
             if e >= 1:
                 make_da1(e - 1)
             if e + 2 < E:
                 load_acts(e + 2)
                 if e in (0, 2):
-                    load_gate(e + 4, 2)
                     load_w2(e // 2 + 2, nc.sync)
+            if e < 4:
+                load_gate(e + 4)
+            if 1 <= e < E - 1:
+                weave_g(e + 1)
+            if e >= 2:
+                store_dx(e - 2)
             if e < E:
                 make_da3(e)
             if e + 1 < E:
-                sig(e + 1)
                 make_y(e + 1)
+            gather_some(quota[e])
             if e >= 1:
                 second_product(e - 1)
-            if e + 3 < E:
-                new_g32(e + 3)
-                for t in range(PACK):
-                    gather(e + 3, t)
             if e + 2 < E:
-                weave_g(e + 2)
+                sig(e + 2)
             if e % 2 == 1 and e + 1 < E:
                 permute_words((e + 1) // 2)
             if e + 1 < E:
                 first_product(e + 1)
+        store_dx(E - 1)
 
         for c in range(T // C):
             ls = slice(c * C // 16, (c + 1) * C // 16)
             r = ring.tile([P, PACK, C], F32, bufs=3, name="g32")
             nc.vector.tensor_copy(r[:, 0, :], dx[:].indirect(l_pos1[:, ls]))
             nc.vector.tensor_copy(r[:, 1, :], dx[:].indirect(l_pos2[:, ls]))
-            eng = nc.vector if c == T // C - 1 else nc.gpsimd
-            eng.tensor_tensor(r[:, 2, :], r[:, 0, :], r[:, 1, :], ADD)
-            nc.sync.dma_start(out[:, c * C : (c + 1) * C], r[:, 2, :])
+            if c < T // C - 1:
+                nc.gpsimd.tensor_tensor(r[:, 2, :], r[:, 0, :], r[:, 1, :], ADD)
+                nc.sync.dma_start(out[:, c * C : (c + 1) * C], r[:, 2, :])
+            else:
+                half = C // 2
+                for h in range(2):
+                    hs = slice(h * half, (h + 1) * half)
+                    nc.vector.tensor_tensor(r[:, 2, hs], r[:, 0, hs], r[:, 1, hs], ADD)
+                    nc.sync.dma_start(out[:, c * C + h * half : c * C + (h + 1) * half], r[:, 2, hs])

@@ -21,7 +21,7 @@ P = 128
 K, T, E, C, H, N = 128, 2048, 8, 512, 512, 512
 S = E * C
 PACK = 4
-Y_GPSIMD = 4
+Y_GPSIMD = 2
 
 FLOPS = 2 * S * (N * H + 2 * H * K)
 BYTES = 4 * (N * T + 2 * H * S + S + K * T) + E * (N * H + 2 * H * K) * 17 // 32 + 2 * P * (S + 2 * T) // 16
@@ -91,9 +91,9 @@ def tile_moe_bdx_glu_sigmoid_kernel(
             )
             w2_raws[pair] = raw
 
-        load_w2(0, nc.scalar)
         for t in range(1, PACK - 1):
             nc.sync.dma_start(dy[t][:], dy_rows[:, t, :])
+        load_w2(0, nc.sync)
 
         a1_rows = a1.rearrange("(p t) c -> p t c", t=PACK)
         a3_rows = a3.rearrange("(p t) c -> p t c", t=PACK)
@@ -166,14 +166,20 @@ def tile_moe_bdx_glu_sigmoid_kernel(
             packed[e] = gb
             nc.scalar.copy(woven(gb[:]), planes(g32s[e][:]))
 
-        def quantize(values, name):
-            cd = ring.tile([P, values.shape[1] // PACK], U32, align_bytes=64, name=f"c_{name}")
-            sc = ring.tile([P, values.shape[1] // PACK], U8, align_bytes=64, name=f"s_{name}")
-            nc.vector.quantize_mx(out=cd[:].bitcast(E5M2X4), scales=sc[:], in_=values)
+        def quantize(values, calls, name):
+            columns = values.shape[1] // PACK
+            cd = ring.tile([P, columns], U32, align_bytes=64, name=f"c_{name}")
+            sc = ring.tile([P, columns], U8, align_bytes=64, name=f"s_{name}")
+            step = columns // calls
+            for c in range(0, columns, step):
+                cs = slice(c, c + step)
+                nc.vector.quantize_mx(
+                    out=cd[:, cs].bitcast(E5M2X4), scales=sc[:, cs], in_=values[:, c * PACK : (c + step) * PACK]
+                )
             return cd, sc
 
         def first_product(e):
-            cd, sc = quantize(packed[e][:].rearrange("p c t -> p (c t)"), "g")
+            cd, sc = quantize(packed[e][:].rearrange("p c t -> p (c t)"), 1, "g")
             out_banks = []
             for t in range(PACK):
                 bank = psum_h.tile([P, C], F32, name="bank")
@@ -199,8 +205,13 @@ def tile_moe_bdx_glu_sigmoid_kernel(
             y_tiles[e] = y_t
             for t in range(0, PACK, 2):
                 ts = slice(t, t + 2)
-                eng = nc.gpsimd if t < Y_GPSIMD else nc.vector
-                eng.tensor_tensor(y_t[:, ts, :], s_tiles[e][:, ts, :], a3_tiles[e][:, ts, :], MULT)
+                if t < Y_GPSIMD and e >= 2:
+                    nc.gpsimd.tensor_tensor(y_t[:, ts, :], s_tiles[e][:, ts, :], a3_tiles[e][:, ts, :], MULT)
+
+        def finish_y(e):
+            y_t = y_tiles[e]
+            ts = slice(Y_GPSIMD if e >= 2 else 0, PACK)
+            nc.vector.tensor_tensor(y_t[:, ts, :], s_tiles[e][:, ts, :], a3_tiles[e][:, ts, :], MULT)
 
         def make_da3(e):
             d3 = ring.tile([P, PACK, C], F32, name="d3")
@@ -216,7 +227,7 @@ def tile_moe_bdx_glu_sigmoid_kernel(
 
         def second_product(e):
             acc = psum_x.tile([P, C], F32, name="acc")
-            cd, sc = quantize(da3s[e][1][:].rearrange("p w c t -> p (w c t)"), "d")
+            cd, sc = quantize(da3s[e][1][:].rearrange("p w c t -> p (w c t)"), 2 if e == E - 1 else 1, "d")
             for w in range(2):
                 cs = slice(w * C, (w + 1) * C)
                 w0 = (w * E + e) * 2 * K
@@ -235,17 +246,18 @@ def tile_moe_bdx_glu_sigmoid_kernel(
         def store_dx(e):
             nc.scalar.activation(dx[:, e * C : (e + 1) * C], accs[e][:], COPY, scale=-1.0)
 
-        permute_scales(0, E)
         for e in range(3):
             new_g32(e)
         for t in range(PACK):
             for e in range(3):
                 gather(e, t)
         sig(0)
+        permute_scales(0, E)
         permute_words(0)
         weave_g(0)
         make_y(0)
         first_product(0)
+        finish_y(0)
         weave_g(1)
         sig(1)
 
@@ -278,15 +290,17 @@ def tile_moe_bdx_glu_sigmoid_kernel(
                 make_da3(e)
             if e + 1 < E:
                 make_y(e + 1)
-            gather_some(quota[e])
+            gather_some(quota[e] // 2)
             if e >= 1:
                 second_product(e - 1)
-            if e + 2 < E:
-                sig(e + 2)
-            if e % 2 == 1 and e + 1 < E:
-                permute_words((e + 1) // 2)
             if e + 1 < E:
                 first_product(e + 1)
+                finish_y(e + 1)
+            gather_some(quota[e] - quota[e] // 2)
+            if e + 2 < E:
+                sig(e + 2)
+            if e % 2 == 0 and e + 2 < E:
+                permute_words(e // 2 + 1)
         store_dx(E - 1)
 
         for c in range(T // C):

from contextlib import ExitStack

import concourse.mybir as mybir

F32 = mybir.dt.float32
BF16 = mybir.dt.bfloat16
I32 = mybir.dt.int32
U32 = mybir.dt.uint32
U16 = mybir.dt.uint16
U8 = mybir.dt.uint8
E5M2X4 = mybir.dt.float8_e5m2_x4
E2M1X4 = mybir.dt.float4_e2m1fn_x4

MULT = mybir.AluOpType.mult
ADD = mybir.AluOpType.add
SUB = mybir.AluOpType.subtract
COPY = mybir.ActivationFunctionType.Copy
SIGMOID = mybir.ActivationFunctionType.Sigmoid

P = 128
K, T, E, C, H, N = 128, 2048, 8, 512, 512, 512
S = E * C
PACK = 4
Y_GPSIMD = 2

FLOPS = 2 * S * (N * H + 2 * H * K)
BYTES = 4 * (N * T + 2 * H * S + S + K * T) + E * (N * H + 2 * H * K) * 17 // 32 + 2 * P * (S + 2 * T) // 16


def planes(ap):
    return ap.rearrange("p t (c i) -> p c t i", i=4)


def woven(ap):
    return ap.rearrange("p (c i) t -> p c t i", i=4)


def tile_moe_bdx_glu_sigmoid_kernel(
    tc, dyT, a1, a3, w2_words, w2_scales, w1_words, w1_scales, w3_words, w3_scales, gate, offs, pos1, pos2, out
):
    nc = tc.nc
    with ExitStack() as ctx:
        lists = ctx.enter_context(tc.tile_pool(name="lists", bufs=1))
        held = ctx.enter_context(tc.tile_pool(name="held", bufs=1))
        acts = ctx.enter_context(tc.tile_pool(name="acts", bufs=3))
        ring = ctx.enter_context(tc.tile_pool(name="ring", bufs=2))
        psum_h = ctx.enter_context(tc.psum_pool(name="psum_h", bufs=6))
        psum_x = ctx.enter_context(tc.psum_pool(name="psum_x", bufs=2))

        l_offs = lists.tile([P, S // 16], U16, name="l_offs")
        l_pos1 = lists.tile([P, T // 16], U16, name="l_pos1")
        l_pos2 = lists.tile([P, T // 16], U16, name="l_pos2")

        dy = [held.tile([P, T], F32, name=f"dy{t}") for t in range(PACK)]
        gates = held.tile([P, S], F32, name="gates")
        dx = held.tile([P, S], F32, name="dx")
        w2_sraw = held.tile([P, E * H], U8, align_bytes=64, name="w2_sraw")
        w2_w = held.tile([P, E * 2 * H], U8, align_bytes=64, name="w2_w")
        w2_s = held.tile([P, E * H], U8, align_bytes=64, name="w2_s")
        w13_w = held.tile([P, 2 * E * 2 * K], U8, align_bytes=64, name="w13_w")
        w13_s = held.tile([P, 2 * E * K], U8, align_bytes=64, name="w13_s")

        nc.gpsimd.memset(w2_sraw[:].bitcast(I32), 0)
        nc.gpsimd.memset(w13_s[:].bitcast(I32), 0)

        nc.sync.dma_start(l_offs[:], offs)
        dy_rows = dyT.rearrange("(p t) c -> p t c", t=PACK)

        def load_gate(e):
            cols = slice(e * C, (e + 1) * C)
            nc.sync.dma_start(gates[:, cols], gate[0:P, cols])

        load_gate(0)
        nc.sync.dma_start(dy[0][:], dy_rows[:, 0, :])
        load_gate(1)
        load_gate(2)

        w2s_view = w2_sraw[:].bitcast(I32).rearrange("p (e i) -> p e i", e=E)
        w2s_dram = w2_scales.bitcast(I32)
        for q in range(4):
            nc.scalar.dma_start(
                w2s_view[32 * q : 32 * q + 4], w2s_dram[:, 0, 4 * q : 4 * q + 4, :].rearrange("e f i -> f e i")
            )
        w2_raws = {}

        def load_w2(pair, queue):
            raw = ring.tile([P, 2 * 2 * H], U8, align_bytes=64, name="w2_raw")
            queue.dma_start(
                raw[:].bitcast(I32).rearrange("p (e i) -> p e i", e=2),
                w2_words.bitcast(I32)[2 * pair : 2 * pair + 2, 0].rearrange("e p i -> p e i"),
            )
            w2_raws[pair] = raw

        for t in range(1, PACK - 1):
            nc.sync.dma_start(dy[t][:], dy_rows[:, t, :])
        load_w2(0, nc.sync)

        a1_rows = a1.rearrange("(p t) c -> p t c", t=PACK)
        a3_rows = a3.rearrange("(p t) c -> p t c", t=PACK)
        s_tiles = {}
        a3_tiles = {}
        y_tiles = {}

        def load_acts(e):
            cols = slice(e * C, (e + 1) * C)
            s_t = acts.tile([P, PACK, C], F32, name="s_t")
            nc.sync.dma_start(s_t[:], a1_rows[:, :, cols])
            if e == 0:
                nc.sync.dma_start(dy[PACK - 1][:], dy_rows[:, PACK - 1, :])
            a3_t = acts.tile([P, PACK, C], F32, bufs=2, name="a3_t")
            nc.sync.dma_start(a3_t[:], a3_rows[:, :, cols])
            s_tiles[e] = s_t
            a3_tiles[e] = a3_t

        load_acts(0)
        w13w_view = w13_w[:].bitcast(I32).rearrange("p (w e i) -> p w e i", w=2, e=E)
        w13s_view = w13_s[:].bitcast(I32).rearrange("p (w e i) -> p w e i", w=2, e=E)
        for w, (words, scales) in enumerate(((w1_words, w1_scales), (w3_words, w3_scales))):
            nc.sync.dma_start(w13w_view[:, w], words.bitcast(I32)[:, 0].rearrange("e p i -> p e i"))
            s_dram = scales.bitcast(I32)
            for q in range(4):
                nc.sync.dma_start(
                    w13s_view[32 * q : 32 * q + 4, w], s_dram[:, 0, 4 * q : 4 * q + 4, :].rearrange("e f i -> f e i")
                )
        load_w2(1, nc.sync)
        load_gate(3)
        load_acts(1)
        nc.sync.dma_start(l_pos1[:], pos1)
        nc.sync.dma_start(l_pos2[:], pos2)

        def permute_scales(e0, e1):
            cs = slice(e0 * H, e1 * H)
            nc.vector.tensor_copy(
                w2_s[:, cs].rearrange("p (e t m) -> p e t m", e=e1 - e0, t=PACK),
                w2_sraw[:, cs].rearrange("p (e m t) -> p e t m", e=e1 - e0, t=PACK),
            )

        def permute_words(pair):
            cs = slice(pair * 4 * H, (pair + 1) * 4 * H)
            nc.vector.tensor_copy(
                w2_w[:, cs].bitcast(U16).rearrange("p (e t m) -> p e t m", e=2, t=PACK),
                w2_raws[pair][:].bitcast(U16).rearrange("p (e m t) -> p e t m", e=2, t=PACK),
            )

        g32s = {}
        codes = {}
        banks = {}
        da3s = {}
        packed = {}
        accs = {}

        def new_g32(e):
            g32 = ring.tile([P, PACK, C], F32, bufs=3, name="g32")
            g32s[e] = g32

        def gather(e, t):
            nc.vector.tensor_tensor(
                g32s[e][:, t, :],
                dy[t][:].indirect(l_offs[:, e * C // 16 : (e + 1) * C // 16]),
                gates[:, e * C : (e + 1) * C],
                MULT,
            )

        def weave_g(e):
            gb = ring.tile([P, C, PACK], BF16, align_bytes=64, name="gb")
            packed[e] = gb
            nc.scalar.copy(woven(gb[:]), planes(g32s[e][:]))

        def quantize(values, calls, name):
            columns = values.shape[1] // PACK
            cd = ring.tile([P, columns], U32, align_bytes=64, name=f"c_{name}")
            sc = ring.tile([P, columns], U8, align_bytes=64, name=f"s_{name}")
            step = columns // calls
            for c in range(0, columns, step):
                cs = slice(c, c + step)
                nc.vector.quantize_mx(
                    out=cd[:, cs].bitcast(E5M2X4), scales=sc[:, cs], in_=values[:, c * PACK : (c + step) * PACK]
                )
            return cd, sc

        def first_product(e):
            cd, sc = quantize(packed[e][:].rearrange("p c t -> p (c t)"), 1, "g")
            out_banks = []
            for t in range(PACK):
                bank = psum_h.tile([P, C], F32, name="bank")
                w0 = e * 2 * H + t * 2 * P
                s0 = e * H + t * P
                nc.tensor.matmul_mx(
                    out=bank[:],
                    lhsT=w2_w[:, w0 : w0 + 2 * P].bitcast(E2M1X4),
                    lhsT_scale=w2_s[:, s0 : s0 + P],
                    rhs=cd[:].bitcast(E5M2X4),
                    rhs_scale=sc[:],
                    start=True,
                    stop=True,
                )
                out_banks.append(bank)
            banks[e] = out_banks

        def sig(e):
            nc.scalar.activation(s_tiles[e][:], s_tiles[e][:], SIGMOID, scale=-1.0)

        def make_y(e):
            y_t = acts.tile([P, PACK, C], F32, bufs=2, name="y_t")
            y_tiles[e] = y_t
            for t in range(0, PACK, 2):
                ts = slice(t, t + 2)
                if t < Y_GPSIMD and e >= 2:
                    nc.gpsimd.tensor_tensor(y_t[:, ts, :], s_tiles[e][:, ts, :], a3_tiles[e][:, ts, :], MULT)

        def finish_y(e):
            y_t = y_tiles[e]
            ts = slice(Y_GPSIMD if e >= 2 else 0, PACK)
            nc.vector.tensor_tensor(y_t[:, ts, :], s_tiles[e][:, ts, :], a3_tiles[e][:, ts, :], MULT)

        def make_da3(e):
            d3 = ring.tile([P, PACK, C], F32, name="d3")
            for t in range(PACK):
                nc.vector.scalar_tensor_tensor(d3[:, t, :], s_tiles[e][:, t, :], 1.0, banks[e][t][:], SUB, MULT)
            db = ring.tile([P, 2, C, PACK], BF16, align_bytes=64, name="db")
            nc.scalar.copy(woven(db[:, 1]), planes(d3[:]))
            da3s[e] = (d3, db)

        def make_da1(e):
            d3, db = da3s[e]
            nc.vector.tensor_tensor(woven(db[:, 0]), planes(y_tiles[e][:]), planes(d3[:]), MULT)

        def second_product(e):
            acc = psum_x.tile([P, C], F32, name="acc")
            cd, sc = quantize(da3s[e][1][:].rearrange("p w c t -> p (w c t)"), 2 if e == E - 1 else 1, "d")
            for w in range(2):
                cs = slice(w * C, (w + 1) * C)
                w0 = (w * E + e) * 2 * K
                s0 = (w * E + e) * K
                nc.tensor.matmul_mx(
                    out=acc[:],
                    lhsT=w13_w[:, w0 : w0 + 2 * K].bitcast(E2M1X4),
                    lhsT_scale=w13_s[:, s0 : s0 + K],
                    rhs=cd[:, cs].bitcast(E5M2X4),
                    rhs_scale=sc[:, cs],
                    start=(w == 0),
                    stop=(w == 1),
                )
            accs[e] = acc

        def store_dx(e):
            nc.scalar.activation(dx[:, e * C : (e + 1) * C], accs[e][:], COPY, scale=-1.0)

        for e in range(3):
            new_g32(e)
        for t in range(PACK):
            for e in range(3):
                gather(e, t)
        sig(0)
        permute_scales(0, E)
        permute_words(0)
        weave_g(0)
        make_y(0)
        first_product(0)
        finish_y(0)
        weave_g(1)
        sig(1)

        todo = [(e, t) for e in range(3, E) for t in range(PACK)]

        def gather_some(count):
            for e, t in todo[:count]:
                if t == 0:
                    new_g32(e)
                gather(e, t)
            del_count = min(count, len(todo))
            for i in range(del_count):
                todo.remove(todo[0])

        quota = (4, 3, 3, 3, 3, 4, 0, 0, 0)
        for e in range(E + 1):
            if e >= 1:
                make_da1(e - 1)
            if e + 2 < E:
                load_acts(e + 2)
                if e in (0, 2):
                    load_w2(e // 2 + 2, nc.sync)
            if e < 4:
                load_gate(e + 4)
            if 1 <= e < E - 1:
                weave_g(e + 1)
            if e >= 2:
                store_dx(e - 2)
            if e < E:
                make_da3(e)
            if e + 1 < E:
                make_y(e + 1)
            gather_some(quota[e] // 2)
            if e >= 1:
                second_product(e - 1)
            if e + 1 < E:
                first_product(e + 1)
                finish_y(e + 1)
            gather_some(quota[e] - quota[e] // 2)
            if e + 2 < E:
                sig(e + 2)
            if e % 2 == 0 and e + 2 < E:
                permute_words(e // 2 + 1)
        store_dx(E - 1)

        for c in range(T // C):
            ls = slice(c * C // 16, (c + 1) * C // 16)
            r = ring.tile([P, PACK, C], F32, bufs=3, name="g32")
            nc.vector.tensor_copy(r[:, 0, :], dx[:].indirect(l_pos1[:, ls]))
            nc.vector.tensor_copy(r[:, 1, :], dx[:].indirect(l_pos2[:, ls]))
            if c < T // C - 1:
                nc.gpsimd.tensor_tensor(r[:, 2, :], r[:, 0, :], r[:, 1, :], ADD)
                nc.sync.dma_start(out[:, c * C : (c + 1) * C], r[:, 2, :])
            else:
                half = C // 2
                for h in range(2):
                    hs = slice(h * half, (h + 1) * half)
                    nc.vector.tensor_tensor(r[:, 2, hs], r[:, 0, hs], r[:, 1, hs], ADD)
                    nc.sync.dma_start(out[:, c * C + h * half : c * C + (h + 1) * half], r[:, 2, hs])
